import numpy as np, ml_dtypes
CORES = [242,247,114,119]
N = 4
BF = ml_dtypes.bfloat16
def gentries(a):
    return np.ascontiguousarray(a.reshape(8, 16, -1).transpose(0, 2, 1)).reshape(8, -1)
def gtable(e):
    e = np.asarray(e); return np.ascontiguousarray(e.reshape(8, -1, 16).transpose(0, 2, 1)).reshape(128, -1).astype(np.int32)
P, BS, T, CAP, G = 2368, 256, 4, 160, 128
S, SB, NEED, KILL = 2, 1, 8, 3
W = P + (N - 1) * G
def clans(rng, kk):
    sc = rng.choice(np.array([191.0, 120.0, 60.0], np.float32), (8, 1, 1)); cen = (sc * rng.random((8, 16, 4))).astype(np.float32); cen[:, :, 0] *= np.float32(0.1)
    t = np.maximum(1, (sc * (0.06 + 0.08 * rng.random((N, 8, 16, 1)))).astype(np.int32)); off = rng.integers(0, 4, (8, 1))
    def near():
        who = ((rng.random((N, 8, P)) * kk[:, None]).astype(np.int64) + off) & 3
        w = sc * (np.float32(0.05) + np.float32(0.15) * rng.random((N, 8, 1, P), dtype=np.float32))
        v = np.take_along_axis(np.broadcast_to(cen, (N, 8, 16, 4)), who[:, :, None, :], 3) + w * (2 * rng.random((N, 8, 16, P), dtype=np.float32) - 1)
        return np.clip(np.rint(v), 0, 191).astype(np.int32)
    x = near(); share = KILL * kk[:, None, None] * rng.choice(np.array([0.03, 0.06, 0.09]), (N, 8, 1, 1))
    y = np.where(rng.random((N, 8, 1, P)) < 0.1, 255, rng.integers(0, 192, (N, 8, 16, P), dtype=np.int32))
    return x, np.where(rng.random((N, 8, 1, P)) < share, near(), y), t
def chosen(key):
    return np.ascontiguousarray(np.argsort(key, axis=-1)[..., :16 * BS])
def deal(pts, num):
    a = np.empty((16, BS), np.int64); a[:, pts] = num.reshape(BS, 16).T
    return a.reshape(-1)
def parts(rng):
    x, y, t = clans(rng, rng.permutation(np.array([1, 1, 2, 2, 2, 3, 3, 4])))
    sd = rng.random((N, 8, BS)) < rng.choice(np.array([0.2, 0.4, 0.6, 0.9]), (N, 8, 1))
    c = chosen(rng.random((N, 8, T, S * W), dtype=np.float32))
    b = np.argsort(rng.random((N, 8, P)) * np.where(np.arange(P) < T * BS, 0.6, 1.0), axis=-1)[..., :(N - 1) * G]
    return x, y, t, sd, c, np.ascontiguousarray(b)
def pack(x, y, t, sd, c, b):
    c = c.reshape(N, 8, T, 16, BS).transpose(0, 1, 3, 2, 4).reshape(N, 128, T * BS)
    return {"x": x.reshape(N, 128, P).astype(np.float32).astype(BF), "y0": y.reshape(N, 128, P).astype(np.float32).astype(BF),
            "tl": t.reshape(N, 128, 1).astype(np.float32).astype(BF), "sd": sd.astype(np.float32).astype(BF),
            "cd": np.ascontiguousarray(c).astype(np.int32), "snd": np.stack([gtable(a) for a in b])}
def setup_inputs(rng):
    return pack(*parts(rng))
def setup_inputs_room(rng):
    x, y, t, sd, c, b = parts(rng)
    o = np.argsort(np.argsort(rng.random((N, 8, BS)), axis=-1), axis=-1); n = rng.choice(np.array([0, 1, CAP - 1, CAP, CAP + 1, BS]), (N, 8))
    n[0] = (CAP, CAP + 1, BS, CAP - 1, 1, 0, CAP, BS); n[1] = (BS, CAP, CAP + 1, CAP, CAP - 1, CAP, 0, 1)
    return pack(x, y, t, o < n[..., None], c, b)
def setup_inputs_ties(rng):
    x, y, t, sd, c, b = parts(rng)
    t = np.tile(rng.integers(0, 21, (1, 8, 16, 1)), (N, 1, 1, 1)); base = rng.integers(10, 121, (8, 16, 1))
    def step():
        return base + t * rng.integers(0, 3, (N, 8, 16, P), dtype=np.int32) + (rng.random((N, 8, 16, P), dtype=np.float32) < 0.3)
    x = step(); y = np.where(rng.random((N, 8, 1, P)) < 0.1 * KILL, step(), 255)
    t[:, 0] = 63; x[:, 0] = rng.choice(np.array([127, 128, 191]), (N, 16, P)); y[:, 0] = rng.choice(np.array([255, 255, 255, 191, 128, 64]), (N, 16, P))
    return pack(x, y, t, sd, c, b)
def setup_inputs_ends(rng):
    x, y, t, sd, c, b = parts(rng); a = np.arange(S * W); n = np.arange(BS); k = np.arange((N - 1) * G)
    key = rng.random((N, 8, T, S * W), dtype=np.float32)
    key[:, 1::2, :, S * P:] -= 1; key[:, 1::2, :, :S] -= 1; key[:, 1::2, :, S * (P - 1):S * P] -= 1
    key[:, 2] += (a >= 16 * BS).astype(np.float32); key[:, 4] += (a < S * W - 16 * BS).astype(np.float32)
    c = rng.permuted(chosen(key), axis=-1); c[:, 6] = np.arange(16 * BS)
    b[:, 1] = k; b[:, 3] = P - 1 - k; b[:, 7] = T * BS - (N - 1) * G + k
    sd[:, ::2] = n >= BS - CAP; sd[:, 1::2] = (n & 1) == 0; sd[:, 5] = (n == 0) | (n == BS - 1)
    return pack(x, y, t, sd, c, b)
def setup_inputs_dark(rng):
    x, y, t, sd, c, b = parts(rng); q = rng.permutation(N); g = rng.permutation(8)
    y[:, g[1]] = 255; t[:, g[2]] = 0
    for j in g[3:7]:
        x[:, j] = x[:, j] & 31; t[:, j] = 63
    y[:, g[3]] = y[:, g[3]] & 31; y[:, g[4]] = 128 + (y[:, g[4]] & 63)
    for r in range(N):
        m = np.isin(np.arange(BS) & 15, rng.permutation(16)[:16 * CAP // BS]); sd[r, g[4]] = m
        num = np.concatenate([rng.permutation(np.arange(S * P, S * W)), np.arange(16 * BS - S * (W - P))])
        c[r, g[4], 0] = deal(np.argsort(rng.random(BS) - m), num)
        m = rng.permutation(BS) < CAP; sd[r, g[5]] = m; o = rng.permutation(16)
        pl = np.argsort(o[np.arange(W) & 15] + rng.random(W))[:16 * CAP]; num = rng.permutation(S * pl + rng.integers(0, S, 16 * CAP))
        num = np.concatenate([num, rng.permutation(np.setdiff1d(np.arange(S * W), num))])[:16 * BS]
        c[r, g[5], 0] = deal(np.argsort(rng.random(BS) - m), num)
    c[:, g[4], 1:] = rng.permuted(np.tile(np.arange(16 * BS), (N, T - 1, 1)), axis=-1)
    key = rng.random((N, S * W)); key[:, S * BS:2 * S * BS] += 1; c[:, g[6], 0] = chosen(key)
    b[:, g[6]] = np.argsort(rng.random((N, P)) + (np.arange(P) // BS == 1), axis=-1)[:, :(N - 1) * G]
    sd[:, g[0]] = False; sd[q[0]] = False; sd[q[1], g[3]] = True
    return pack(x, y, t, sd, c, b)
def setup_inputs_spread(rng):
    x, y, t, sd, c, b = parts(rng)
    x = np.minimum((np.exp2(7.59 * rng.random((N, 8, 1, P))) * rng.random((N, 8, 16, P))).astype(np.int32), 191)
    y = np.minimum((np.exp2(7.59 * rng.random((N, 8, 1, P))) * rng.random((N, 8, 16, P))).astype(np.int32), 191)
    y = np.where(rng.random((N, 8, 1, P)) < rng.choice(np.array([0.1, 0.5, 0.9]), (N, 8, 1, 1)), 255, y)
    low = np.arange(16)[:, None] == rng.integers(0, 16, (N, 8, 1, P))
    y = np.where(rng.random((N, 8, 1, P)) < 0.15, np.where(low, y >> 3, 255), y)
    t = np.rint(np.exp2(6 * rng.random((N, 8, 16, 1)))).astype(np.int32) - 1
    return pack(x, y, np.minimum(t, 63), rng.random((N, 8, BS)) < rng.random((N, 8, 1)), c, b)
def check_inputs(d):
    bad = []
    for k, hi in (("x", 191), ("y0", 191), ("tl", 63), ("sd", 1)):
        v = np.asarray(d[k]).astype(np.float32); ok = (v >= 0) & (v <= hi) & (v == np.floor(v))
        if k == "y0": ok = ok | (v == 255)
        if not np.all(ok): bad.append("range of " + k)
    for k, hi in (("cd", S * W - 1), ("snd", P - 1)):
        if np.min(d[k]) < 0 or np.max(d[k]) > hi: bad.append("range of " + k)
    c = np.sort(np.asarray(d["cd"]).reshape(N, 8, 16, T, BS).transpose(0, 1, 3, 2, 4).reshape(N, 8, T, 16 * BS), axis=-1)
    if np.any(c[..., 1:] == c[..., :-1]): bad.append("equal numbers in a brood of cd")
    s = np.sort(np.stack([gentries(a) for a in d["snd"]]), axis=-1)
    if np.any(s[..., 1:] == s[..., :-1]): bad.append("equal numbers in snd")
    return bad
def windows(a, sl):
    res = []
    for r in range(N):
        w = [a[r]]
        for d in range(1, N):
            q = (r - d) % N; w.append(np.take_along_axis(a[q], sl[q, :, d - 1][:, None, :], 2))
        res.append(np.concatenate(w, axis=2))
    return np.stack(res)
def matches(come, xn, t):
    return np.add.reduce((np.abs(come - xn[:, None, :]) <= t[:, :, None]).astype(np.int64), axis=0) >= NEED
def reference(x, y0, tl, sd, cd, snd):
    X = x.astype(np.float32).astype(np.int32).reshape(N, 8, 16, P); Y = y0.astype(np.float32).astype(np.int32).reshape(N, 8, 16, P)
    t = tl.astype(np.float32).astype(np.int32).reshape(N, 8, 16, 1)
    C = (cd.astype(np.int64) >> SB).reshape(N, 8, 16, T * BS); sl = np.stack([gentries(a) for a in snd]).astype(np.int64).reshape(N, 8, N - 1, G)
    flag = np.zeros((N, 8, P), bool); flag[:, :, :BS] = sd.astype(np.float32) > 0.5; member = np.zeros((N, 8, P), bool)
    xw = windows(X, sl)
    for s in range(T):
        fl = flag[:, :, s * BS:(s + 1) * BS]
        member[:, :, s * BS:(s + 1) * BS] = fl & (np.add.accumulate(fl.astype(np.int64), axis=2) <= CAP)
        new = np.zeros((N, 8, W), bool)
        for r in range(N):
            for g in range(8):
                n = np.flatnonzero(member[r, g, s * BS:(s + 1) * BS]) + s * BS; c = C[r, g][:, n]
                come = xw[r, g][:, c.reshape(-1)].reshape(16, 16, len(n))
                new[r, g][c[matches(come, X[r, g][:, n], t[r, g])]] = True
        for r in range(N):
            flag[r] |= new[r, :, :P]
            for d in range(1, N):
                q = (r - d) % N
                for g in range(8): flag[q, g, sl[q, g, d - 1][new[r, g, P + (d - 1) * G:P + d * G]]] = True
    for s in range(T - 1, -1, -1):
        yw = windows(Y, sl); Z = Y.copy()
        for r in range(N):
            for g in range(8):
                n = np.flatnonzero(member[r, g, s * BS:(s + 1) * BS]) + s * BS; c = C[r, g][:, n]; xn = X[r, g][:, n]
                come = yw[r, g][:, c.reshape(-1)].reshape(16, 16, len(n))
                dead = np.add.reduce(matches(come, xn, t[r, g]).astype(np.int64), axis=0) >= KILL
                Z[r, g][:, n] = np.where(dead, 255, (xn + np.minimum(191, np.minimum.reduce(come, axis=1))) >> 1)
        Y = Z
    return {"yv": np.ascontiguousarray(Y[:, :, :, :T * BS]).reshape(N, 128, T * BS).astype(np.float32).astype(BF), "yf": np.where(member, 2, flag.astype(np.int64)).astype(np.float32).astype(BF)}

from concourse.bass import DstId, RemoteDMATransfer
from concourse.mybir import AluOpType as OP, ActivationFunctionType as AF

N, P, BS, T4, CAP, GB, S2 = 4, 2368, 256, 4, 160, 128, 2
NB = (N - 1) * GB
W = P + NB
ST = S2 * W
MA = 96
MB = CAP - MA
EA, EB, E = 16 * MA, 16 * MB, 16 * CAP
SWN = 2 * ST + E
VS, VS3 = 88, 76
SIN = 16 * 96
SLOT = 768
XSH = 14
XDEF = 512
LW = 148

SCRATCH = {
    "xw": ("sbuf", [128, W], "bfloat16"), "yw": ("sbuf", [128, P + 4 * NB], "bfloat16"),
    "cdw": ("sbuf", [128, T4 * BS], "int32"), "snd32": ("sbuf", [128, NB // 16], "int32"),
    "sndw": ("sbuf", [128, NB // 16], "uint16"), "tlc": ("sbuf", [128, 1], "bfloat16"), "sdrow": ("sbuf", [128, BS], "bfloat16"),
    "swv": ("sbuf", [128, SWN], "bfloat16"), "sws": ("sbuf", [128, SWN], "float32"),
    "swc": ("sbuf", [128, 2 * P], "bfloat16"), "swb": ("sbuf", [128, 2 * NB], "bfloat16"), "swo": ("sbuf", [128, 2 * BS], "bfloat16"),
    "ones": ("sbuf", [128, 16], "bfloat16"), "sin": ("sbuf", [128, SIN], "float32"),
    "come": ("sbuf", [128, E], "bfloat16"), "ab": ("sbuf", [128, E], "bfloat16"), "ind": ("sbuf", [128, E], "bfloat16"),
    "mn": ("sbuf", [128, E], "bfloat16"), "d0": ("sbuf", [128, E], "bfloat16"),
    "pk": ("sbuf", [128, T4 * BS], "int32"), "pkc": ("sbuf", [128, T4 * SLOT], "int32"),
    "pkd0": ("sbuf", [128, CAP], "int32"), "pkd": ("sbuf", [128, CAP], "int32"),
    "sel": ("sbuf", [128, 16 * 128], "bfloat16"), "qp": ("sbuf", [128, 128], "bfloat16"), "bd": ("sbuf", [128, 128], "bfloat16"),
    "tri": ("sbuf", [128, 128], "bfloat16"), "idn": ("sbuf", [128, 128], "bfloat16"), "idx": ("sbuf", [128, 128], "bfloat16"),
    "pmi": ("sbuf", [128, 1], "int32"), "pm2": ("sbuf", [128, 1], "int32"), "pmod": ("sbuf", [128, 1], "float32"),
    "nmod": ("sbuf", [128, BS], "bfloat16"), "mask": ("sbuf", [128, BS], "bfloat16"), "seg0": ("sbuf", [128, BS], "bfloat16"),
    "c16": ("sbuf", [128, 16], "float32"), "nrow": ("sbuf", [128, 16], "bfloat16"), "nc": ("sbuf", [128, 16], "float32"),
    "i384": ("sbuf", [128, NB], "bfloat16"), "bp": ("sbuf", [128, P], "bfloat16"), "bposw": ("sbuf", [128, 48], "uint16"),
    "fw": ("sbuf", [128, 64], "bfloat16"), "fb": ("sbuf", [128, BS], "bfloat16"), "fsc": ("sbuf", [128, BS], "bfloat16"),
    "nown": ("sbuf", [128, 64], "bfloat16"), "cs": ("sbuf", [128, 32], "bfloat16"), "tp": ("sbuf", [128, 16], "float32"),
    "of32": ("sbuf", [128, 16], "float32"), "offs": ("sbuf", [128, 64], "uint16"),
    "shf": ("sbuf", [128, T4 * CAP], "int32"), "lst": ("sbuf", [128, T4 * CAP], "uint16"), "lsb": ("sbuf", [128, T4 * CAP], "uint16"),
    "lf": ("sbuf", [128, CAP], "float32"), "lg": ("sbuf", [128, CAP], "float32"),
    "xi": ("sbuf", [128, CAP], "int32"), "xmn": ("sbuf", [128, T4 * CAP], "bfloat16"), "vi": ("sbuf", [128, CAP], "int32"),
    "nq": ("sbuf", [128, CAP], "float32"), "so": ("sbuf", [128, CAP], "float32"), "sof": ("sbuf", [128, CAP], "uint16"),
    "mt": ("sbuf", [128, CAP], "bfloat16"), "dd": ("sbuf", [128, CAP], "float32"), "hs": ("sbuf", [128, CAP], "int32"),
    "hv": ("sbuf", [128, CAP], "int32"), "vals": ("sbuf", [128, T4 * SLOT], "bfloat16"), "yb": ("sbuf", [128, T4 * BS], "bfloat16"),
    "memc": ("sbuf", [128, SLOT], "bfloat16"), "memn": ("sbuf", [128, SLOT], "bfloat16"),
    "memr": ("sbuf", [128, T4 * BS], "bfloat16"), "rw": ("sbuf", [128, P], "bfloat16"),
    "yf1": ("sbuf", [128, LW], "float32"), "yf2": ("sbuf", [128, LW], "float32"), "yfs": ("sbuf", [128, LW], "bfloat16"),
}
EX = ["x", "y0", "f0", "f1", "f2", "f3", "y3", "y2", "y1"]
for _e in EX:
    SCRATCH["msg_" + _e] = ("sbuf", [128, NB], "bfloat16")
for _s in range(4):
    SCRATCH["land%d" % _s] = ("sbuf", [128, NB + 16], "bfloat16")
PSB = ["pb0", "pb1", "pb2", "pb3", "pb4", "psc", "psm", "psf"]
for _b in PSB:
    SCRATCH[_b] = ("psum", [128, 512], "float32")
DMAS = ["dx", "dsnd", "dsd", "dtl", "dcd0", "dcd1", "dy0", "oy0", "oy1", "oy2", "oy3", "oyf", "gcast"]
SEMAPHORES = ["sv", "ss", "st", "sg", "snt"] + DMAS + ["arr_" + _e for _e in EX]


def lanes(src, cores, topo):
    near = [c for c in cores if c != src and c in topo.cores_of(src)]
    far = [c for c in cores if c != src and c not in topo.cores_of(src)]
    res, used = {}, []
    for i, c in enumerate(far):
        e = topo.engines(src, c); k = len(e) // len(far)
        res[c] = e[i * k:(i + 1) * k]; used += e
    for c in near:
        e = [q for q in topo.engines(src, c) if q not in used]
        res[c] = e[:4]; used += res[c]
    return res


def rank_program(g, core, T, topo):
    rank = T.rank_of(core)
    if rank is None:
        return
    cores = T.cores
    qh = {"v": g.vector, "s": g.scalar, "t": g.tensor, "g": g, "y": g.sync}
    qsem = {"v": "sv", "s": "ss", "t": "st", "g": "sg"}
    cnt = {}
    know = {q: {} for q in qh}
    clocks = {}
    acc = {}
    seq = [0]

    def conflicts(q, regs, write):
        out = []
        for name, c0, c1 in regs:
            bank = name in PSB
            for a0, a1, w, aq, tok in acc.get(name, []):
                if bank:
                    if aq != q:
                        out.append(tok)
                elif a0 < c1 and c0 < a1 and (w or write):
                    if aq == q and (not w or q == "t"):
                        continue
                    out.append(tok)
        return out

    def wait_for(q, toks):
        best = {}
        for s, v in toks:
            best[s] = max(best.get(s, 0), v)
        for s, v in sorted(best.items(), key=lambda t: -clocks[t][1]):
            if know[q].get(s, 0) >= v:
                continue
            qh[q].wait_ge(T.sem[s], v)
            for k, x in clocks[(s, v)][0].items():
                know[q][k] = max(know[q].get(k, 0), x)
            know[q][s] = max(know[q].get(s, 0), v)

    def note(q, reads, writes, tok):
        for regs, w in ((reads, False), (writes, True)):
            for name, c0, c1 in regs:
                lst = acc.get(name, [])
                if name in PSB:
                    lst = [a for a in lst if a[3] != q]
                elif w:
                    lst = [a for a in lst if not (c0 <= a[0] and a[1] <= c1)]
                else:
                    lst = [a for a in lst if a[2] or a[3] != q or not (c0 <= a[0] and a[1] <= c1)]
                acc[name] = lst + [(c0, c1, w, q, tok)]

    def token(q, sem, n):
        cnt[sem] = cnt.get(sem, 0) + n
        seq[0] += 1
        c = dict(know[q]) if q is not None else {}
        c[sem] = cnt[sem]
        clocks[(sem, cnt[sem])] = (c, seq[0])
        return (sem, cnt[sem])

    def A(name, c0, c1, step=1):
        return ("op", T[name][:, c0:c1:step] if step != 1 else T[name][:, c0:c1], [(name, c0, c1)], [])

    def I(win, off):
        return ("op", win[1].indirect(off[1]), win[2], off[2])

    def do(q, fn, out, *ins, **kw):
        reads, writes, args = list(out[3]), list(out[2]), [out[1]]
        for x in ins:
            if isinstance(x, tuple):
                reads += x[2] + x[3]; args.append(x[1])
            else:
                args.append(x)
        wait_for(q, conflicts(q, reads, False) + conflicts(q, writes, True))
        f = {"copy": lambda: g.vector.tensor_copy, "tt": lambda: g.vector.tensor_tensor, "ts": lambda: g.vector.tensor_scalar,
             "scan": lambda: g.vector.tensor_tensor_scan, "memset": lambda: g.vector.memset, "act": lambda: g.scalar.activation,
             "mm": lambda: g.tensor.matmul, "iota": lambda: g.iota, "asel": lambda: g.affine_select}[fn]()
        r = f(*args, **kw)
        tok = token(q, qsem[q], 1)
        r.then_inc(T.sem[qsem[q]], 1)
        note(q, reads, writes, tok)

    def dma(q, sem, out_ap, in_ap, reads, writes):
        wait_for(q, conflicts(q, reads, False) + conflicts(q, writes, True))
        qh[q].dma_start(out_ap, in_ap).then_inc(T.sem[sem], 16)
        note(q + "dma", reads, writes, token(q, sem, 16))

    V = lambda fn, out, *a, **k: do("v", fn, out, *a, **k)
    S = lambda out, in_, f, **k: do("s", "act", out, in_, f, **k)
    M = lambda out, l, r, a, b: do("t", "mm", out, l, r, a, b)
    G = lambda fn, out, *a, **k: do("g", fn, out, *a, **k)
    sel = lambda a: A("sel", a * 128, (a + 1) * 128)

    def landing(e):
        if e[0] == "f":
            return "land" + e[1], 0
        if e == "x":
            return "xw", P
        return "yw", P + NB * (3 - int(e[1]) + 1 if e != "y0" else 0)

    def send(e):
        name, c0 = landing(e)
        lan = lanes(core, cores, topo)
        wait_for("g", conflicts("g", [("msg_" + e, 0, NB)], False))
        tr = []
        for d in range(1, N):
            dst = cores[(rank + d) % N] if e[0] != "f" else cores[(rank - d) % N]
            rid, pid = topo.addr(dst, core)
            b = (d - 1) * GB
            tr.append(RemoteDMATransfer(dst_ids=[DstId(rid=rid, pnc=pid)], dma_engine_mask=sum(1 << q for q in lan[dst]),
                                        remote_sem=T.sem["arr_" + e], src=T["msg_" + e][:, b:b + GB], dst=T[name][:, c0 + b:c0 + b + GB]))
            cnt["snt"] = cnt.get("snt", 0) + len(lan[dst])
        g.remote_dma_fused(tr, local_sem=T.sem.snt)

    for e in EX:
        name, c0 = landing(e)
        n = sum(len(lanes(c, cores, topo)[core]) for c in cores if c != core)
        note("net", [], [(name, c0, c0 + NB)], token(None, "arr_" + e, n))

    V("memset", A("sdrow", 0, BS), 0.0)
    H = ST // 2
    V("memset", A("swv", 0, H), 0.0)
    dma("s", "dsnd", T.snd32[:, :], T.snd[:, :], [], [("snd32", 0, NB // 16)])
    dma("y", "dx", T.xw[:, 0:P], T.x[:, :], [], [("xw", 0, P)])
    dma("s", "dtl", T.tlc[:, :], T.tl[:, :], [], [("tlc", 0, 1)])
    dma("s", "dsd", T.sdrow[0:128:16, :], T.sd[:, :], [], [("sdrow", 0, BS)])
    dma("y", "dcd0", T.cdw[:, 0:BS], T.cd[:, 0:BS], [], [("cdw", 0, BS)])
    dma("y", "dy0", T.yw[:, 0:P], T.y0[:, :], [], [("yw", 0, P)])
    dma("y", "dcd1", T.cdw[:, BS:T4 * BS], T.cd[:, BS:T4 * BS], [], [("cdw", BS, T4 * BS)])
    G("iota", A("pmi", 0, 1), [[0, 1]], 0, 1)
    G("iota", A("qp", 0, 128), [[0, 8], [1, 16]], 0, 0, allow_small_or_imprecise_dtypes=True)
    G("asel", A("qp", 0, 128), A("qp", 0, 128), [[-16, 8], [0, 16]], OP.is_ge, -1.0, 0, 1)
    G("asel", A("qp", 0, 128), A("qp", 0, 128), [[16, 8], [0, 16]], OP.is_ge, -1.0, 15, -1)
    G("iota", A("c16", 0, 16), [[16, 16]], 0, 0, allow_small_or_imprecise_dtypes=True)
    G("iota", A("nmod", 0, BS), [[0, 16], [1, 16]], 0, 0, allow_small_or_imprecise_dtypes=True)
    G("iota", A("pkd0", 0, CAP), [[16, CAP]], ST + (XDEF << XSH), 0)
    G("iota", A("i384", 0, NB), [[1, NB]], -(NB // 2), 0, allow_small_or_imprecise_dtypes=True)
    S(A("sws", 0, H), A("swv", 0, H), AF.Copy)
    S(A("sin", 0, SIN), A("swv", 0, SIN), AF.Sigmoid)
    V("ts", A("pm2", 0, 1), A("pmi", 0, 1), 15, None, OP.bitwise_and)
    V("copy", A("pmod", 0, 1), A("pm2", 0, 1))
    pmod = A("pmod", 0, 1)
    for a in range(16):
        V("ts", sel(a), A("qp", 0, 128), float(a), None, OP.is_equal)
    V("ts", A("idn", 0, 128), A("qp", 0, 128), pmod, None, OP.is_equal)
    V("copy", A("sndw", 0, 24), A("snd32", 0, 24))
    V("memset", A("swv", H, ST), 0.0)
    bd, tri, idn = A("bd", 0, 128), A("tri", 0, 128), A("idn", 0, 128)

    def border(e, src, c1):
        h = NB // 2
        V("copy", A("msg_" + e, 0, h), I(A(src, 0, c1), A("sndw", 0, 12)))
        S(A("msg_" + e, h, NB), I(A(src, 0, c1), A("sndw", 12, 24)), AF.Copy)
        send(e)

    border("x", "xw", P)
    G("asel", A("d0", 0, E), A("swv", H, H + E), [[0, CAP], [1, 16]], OP.is_gt, 191.0, 0, 0)
    S(A("sws", H, ST), A("swv", H, ST), AF.Copy)

    def wrap(c1, src, ps):
        tot = 16 * len(src); k = 0
        for name, c0, st in src:
            for a in range(16):
                M(A(ps, 0, c1), sel(a), A(name, c0 + a * st, c0 + (16 * (c1 - 1) + a) * st + 1, 16 * st), k == 0, k == tot - 1)
                k += 1

    def pack(s):
        b = s * BS
        M(A("psf", 0, BS), A("idx", 0, 128), A("xw", b, b + BS), True, True)
        V("tt", A("pk", b, b + BS), A("psf", 0, BS), A("cdw", b, b + BS), OP.add)

    def prefill(s):
        V("copy", A("pkc", s * SLOT, s * SLOT + CAP), A("pkd", 0, CAP))

    def slots(s):
        f, a, b = A("fw", 16 * s, 16 * s + 16), s * CAP, (s + 1) * CAP
        M(A("psm", 0, 16), idn, A("nrow", 0, 16), True, False)
        M(A("psm", 0, 16), tri, f, False, False)
        V("scan", A("cs", 1, 17), A("ones", 0, 16), f, 0.0, OP.mult, OP.add)
        M(A("psm", 0, 16), bd, A("cs", 0, 16), False, True)
        V("tt", A("tp", 0, 16), f, A("nc", 0, 16), OP.mult)
        V("tt", A("of32", 0, 16), A("psm", 0, 16), A("tp", 0, 16), OP.subtract)
        V("ts", A("offs", 16 * s, 16 * s + 16), A("of32", 0, 16), 256.0, None, OP.add)
        V("copy", I(A("pkc", s * SLOT, (s + 1) * SLOT), A("offs", 16 * s, 16 * s + 16)), A("pk", s * BS, (s + 1) * BS))
        k = A("pkc", s * SLOT, s * SLOT + CAP)
        V("ts", A("shf", a, b), k, (1 << XSH) - 1, 1, OP.bitwise_and, OP.logical_shift_right)
        V("ts", A("lst", a, b), A("shf", a, b), float(W - 1), None, OP.min)
        V("ts", A("xi", 0, CAP), k, XSH, None, OP.logical_shift_right)
        V("ts", A("xmn", a, b), A("xi", 0, CAP), -1.0, None, OP.mult)

    def match(s, win, wc, lst, between=None):
        x0 = s * CAP
        V("copy", A("come", 0, EA), I(A(win, 0, wc), A(lst, x0, x0 + MA)))
        S(A("come", EA, E), I(A(win, 0, wc), A(lst, x0 + MA, x0 + CAP)), AF.Copy)
        for base, m0, mc, e0 in ((0, MA, MB, EA), (EB, 0, MA, 0)):
            for i in range(16):
                lo = base + i * mc
                cuts = [lo] + [c for c in range(512, E, 512) if lo < c < lo + mc] + [lo + mc]
                for a, b in zip(cuts[:-1], cuts[1:]):
                    out = A("pb%d" % (a // 512), a % 512, a % 512 + b - a)
                    u, w = a - lo, b - lo
                    M(out, idn, A("xmn", x0 + m0 + u, x0 + m0 + w), True, False)
                    M(out, idn, A("come", e0 + 16 * u + i, e0 + 16 * (w - 1) + i + 1, 16), False, True)
        for k in range(5):
            S(A("ab", 512 * k, 512 * k + 512), A("pb%d" % k, 0, 512), AF.Abs)
        if between:
            between()
        for k in range(5):
            V("ts", A("ind", 512 * k, 512 * k + 512), A("ab", 512 * k, 512 * k + 512), A("tlc", 0, 1), None, OP.is_le)
        for base, m0, mc in ((0, MA, MB), (EB, 0, MA)):
            for i in range(16):
                M(A("psc", m0, m0 + mc), sel(i), A("ind", base + i * mc, base + (i + 1) * mc), i == 0, i == 15)

    def targets(s):
        V("ts", A("nq", 0, CAP), A("psc", 0, CAP), 7.5, float(ST), OP.is_lt, OP.mult)
        V("tt", A("so", 0, CAP), A("nq", 0, CAP), A("vi", 0, CAP), OP.add)
        V("copy", A("sof", 0, CAP), A("so", 0, CAP))

    def numbers(s):
        V("ts", A("vi", 0, CAP), A("pkc", s * SLOT, s * SLOT + CAP), (1 << XSH) - 1, None, OP.bitwise_and)

    def scatter(vs):
        V("copy", I(A("swv", 0, SWN), A("sof", 0, vs)), A("sin", 0, 16 * vs))
        S(I(A("sws", 0, SWN), A("sof", vs, CAP)), A("sin", 0, 16 * (CAP - vs)), AF.Sigmoid)

    def tell(s):
        S(A("swb", 0, 2 * NB), A("sws", 2 * P, ST), AF.Copy)
        ps = A("psc", 0, NB)
        M(ps, idn, A("swb", 0, 2 * NB, 2), True, False)
        M(ps, idn, A("swb", 1, 2 * NB, 2), False, False)
        M(ps, idn, A("swv", 2 * P, ST, 2), False, False)
        M(ps, idn, A("swv", 2 * P + 1, ST, 2), False, True)
        S(A("msg_f%d" % s, 0, NB), ps, AF.Copy)
        send("f%d" % s)

    def keep_y(s):
        b = s * BS
        V("tt", A("yb", b, b + BS), I(A("memn", 0, SLOT), A("offs", 16 * s, 16 * s + 16)), A("yw", b, b + BS), OP.mult)

    def back_list(s):
        a, b = s * CAP, (s + 1) * CAP
        V("ts", A("lg", 0, CAP), A("shf", a, b), float(P), float(NB * (3 - s)), OP.is_ge, OP.mult)
        V("tt", A("lf", 0, CAP), A("shf", a, b), A("lg", 0, CAP), OP.add)
        V("ts", A("lsb", a, b), A("lf", 0, CAP), float(P + NB * (4 - s) - 1), None, OP.min)

    def members(s):
        S(A("memr", s * BS, (s + 1) * BS), I(A("memc", 0, SLOT), A("offs", 16 * s, 16 * s + 16)), AF.Copy)

    def zero(name, c0, c1):
        S(A(name, c0, c1), A("xw", 0, c1 - c0), AF.Copy, scale=0.0)

    wrap(16, [("sdrow", 0, 1)], "psm")
    V("ts", bd, A("qp", 0, 128), 0.0, None, OP.is_ge)
    V("ts", tri, A("qp", 0, 128), pmod, None, OP.is_ge)
    V("ts", A("idx", 0, 128), idn, float(1 << XSH), None, OP.mult)
    V("ts", A("nrow", 0, 16), A("c16", 0, 16), pmod, None, OP.add)
    V("ts", A("nc", 0, 16), A("c16", 0, 16), pmod, 257.0, OP.add, OP.add)
    V("memset", A("cs", 0, 1), 0.0)
    V("memset", A("ones", 0, 16), 1.0)
    V("ts", A("fw", 0, 16), A("psm", 0, 16), 0.5, None, OP.is_ge)
    V("ts", A("pkd", 0, CAP), A("pkd0", 0, CAP), pmod, None, OP.add)
    prefill(0)
    pack(0)
    slots(0)
    numbers(0)
    border("y0", "yw", P)
    V("copy", A("swv", 0, 2 * BS, 2), A("sdrow", 0, BS))
    V("memset", A("bp", BS, 4 * BS), float(NB // 2))
    for s in range(4):
        if s:
            ln = "land%d" % (s - 1)
            V("tt", A("fb", 0, BS), I(A(ln, 0, NB + 16), A("bposw", 16 * (s - 1), 16 * s)), A("mask", 0, BS), OP.mult)
            V("scan", A("fsc", 0, BS), A("seg0", 0, BS), A("fb", 0, BS), 0.0, OP.mult, OP.add)
            V("tt", A("fw", 16 * s, 16 * s + 16), A("fsc", 15, BS, 16), A("nown", 16 * s, 16 * s + 16), OP.is_gt)
            slots(s)
        if s == 3:
            break
        match(s, "xw", W, "lst", (lambda s=s: numbers(s)) if s else None)
        targets(s)
        scatter(VS)
        tell(s)
        S(A("swo", 0, 2 * BS), A("sws", 2 * BS * (s + 1), 2 * BS * (s + 2)), AF.Copy)
        if s == 0:
            V("copy", I(A("bp", 0, P), A("sndw", 0, 24)), A("i384", 0, NB))
            wrap(48, [("bp", BS, 1)], "psf")
            V("ts", A("mask", 0, BS), A("nmod", 0, BS), pmod, None, OP.is_equal)
            V("ts", A("seg0", 0, BS), A("nmod", 0, BS), 0.0, None, OP.not_equal)
            V("ts", A("bposw", 0, 48), A("psf", 0, 48), 1.0 / 16, float(NB // 2), OP.mult, OP.add)
        zero("land%d" % s, NB, NB + 16)
        b = 2 * BS * (s + 1)
        wrap(16, [("swv", b, 2), ("swv", b + 1, 2), ("swo", 0, 2), ("swo", 1, 2)], "psm")
        prefill(s + 1)
        pack(s + 1)
        V("ts", A("nown", 16 * s + 16, 16 * s + 32), A("psm", 0, 16), 0.0, -1.0, OP.is_gt, OP.mult)
        zero("vals", SLOT * s, SLOT * s + SLOT)
        if s == 1:
            for name, u, w in (("memc", 64.0, 0.0), ("memn", 0.0, 1.0)):
                V("memset", A(name, 0, CAP), u)
                V("memset", A(name, CAP, SLOT), w)
        for k in ([], [0, 1], [2])[s]:
            back_list(k)
            keep_y(k)
            members(k)
    for s in range(3, -1, -1):
        def low(s=s):
            V("scan", A("mn", 0, E), A("d0", 0, E), A("come", 0, E), 0.0, OP.max, OP.min)
            if s == 3:
                keep_y(3)
            V("tt", A("hs", 0, CAP), A("mn", 15, E, 16), A("xmn", s * CAP, (s + 1) * CAP), OP.subtract)
            V("ts", A("hv", 0, CAP), A("hs", 0, CAP), 1, None, OP.logical_shift_right)
        match(s, "yw", P + NB * (4 - s), "lst" if s == 3 else "lsb", low)
        if s == 3:
            zero("vals", SLOT * 3, SLOT * 4)
        V("ts", A("mt", 0, CAP), A("psc", 0, CAP), 7.5, None, OP.is_ge)
        M(A("psm", 0, CAP), bd, A("mt", 0, CAP), True, True)
        V("ts", A("dd", 0, CAP), A("psm", 0, CAP), 2.5, 255.0, OP.is_ge, OP.mult)
        V("tt", A("vals", s * SLOT, s * SLOT + CAP), A("dd", 0, CAP), A("hv", 0, CAP), OP.max)
        V("tt", A("yw", s * BS, (s + 1) * BS), I(A("vals", s * SLOT, (s + 1) * SLOT), A("offs", 16 * s, 16 * s + 16)),
          A("yb", s * BS, (s + 1) * BS), OP.add)
        if s:
            border("y%d" % s, "yw", P)
        dma("y", "oy%d" % s, T.yv[:, s * BS:(s + 1) * BS], T.yw[:, s * BS:(s + 1) * BS], [("yw", s * BS, (s + 1) * BS)], [])
        if s == 3:
            match(3, "xw", W, "lst", lambda: numbers(3))
            targets(3)
            members(3)
        elif s == 2:
            scatter(VS3)
            V("memset", A("rw", 0, P), 0.0)
        elif s == 1:
            tell(3)
            dma("g", "gcast", T.swc[:, :], T.sws[:, 0:2 * P], [("sws", 0, 2 * P)], [("swc", 0, 2 * P)])
            for st in range(2):
                for h in range(16):
                    M(A("psf", 0, LW), sel(h), A("swv", 2 * LW * h + st, 2 * LW * (h + 1), 2), st == 0 and h == 0, False)
            for h in range(7):
                n = min(LW, T4 * BS - LW * h)
                M(A("psf", 0, n), sel(h), A("memr", LW * h, LW * h + n), False, False)
    for st in range(2):
        for h in range(16):
            M(A("psf", 0, LW), sel(h), A("swc", 2 * LW * h + st, 2 * LW * (h + 1), 2), False, False)
    V("copy", I(A("rw", 0, P), A("sndw", 0, 24)), A("land3", 0, NB))
    for h in range(16):
        M(A("psf", 0, LW), sel(h), A("rw", LW * h, LW * (h + 1)), False, h == 15)
    V("ts", A("yf1", 0, LW), A("psf", 0, LW), 0.0, None, OP.is_gt)
    V("ts", A("yf2", 0, LW), A("psf", 0, LW), 500.0, None, OP.is_ge)
    V("tt", A("yfs", 0, LW), A("yf1", 0, LW), A("yf2", 0, LW), OP.add)
    dma("y", "oyf", T.yf[:, :], T.yfs[:, :], [("yfs", 0, LW)], [])
    for sname in SEMAPHORES:
        if cnt.get(sname, 0) and know["g"].get(sname, 0) < cnt[sname]:
            g.wait_ge(T.sem[sname], cnt[sname])
